import numpy as np
import ml_dtypes


def mxq(x, axis, fmt="e4m3"):
    dtype, down = {"e4m3": (ml_dtypes.float8_e4m3fn, 7), "e5m2": (ml_dtypes.float8_e5m2, 14)}[fmt]
    v = np.moveaxis(np.asarray(x, np.float32).astype(ml_dtypes.bfloat16).astype(np.float64), axis, -1)
    blocks = v.reshape(v.shape[:-1] + (-1, 32))
    amax = np.abs(blocks).max(-1, keepdims=True)
    byte = np.maximum(np.where(amax > 0, np.frexp(amax)[1] - 1 + 127, 0) - down, 1)
    scale = np.exp2(byte - 127.0)
    codes = (blocks / scale).astype(np.float32).astype(dtype).astype(np.float64)
    return np.moveaxis((codes * scale).reshape(v.shape), -1, axis)


WIDE = False


def mx_kscale(k):
    if not WIDE:
        return np.ones(k)
    levels = np.array([10, -10, 5, -5, 0])
    if k % 512:
        return np.exp2(np.random.permutation(np.resize(levels, k // 32))).repeat(32)
    a = np.empty((k // 512, 16))
    for p in range(k // 512):
        a[p, :8] = np.random.permutation(np.resize(levels, 8))
        for g in range(8):
            far = levels[np.abs(levels - a[p, g]) >= 10]
            a[p, g + 8] = far[np.random.randint(len(far))]
    return np.exp2(a.ravel()).repeat(32)


def f64(x):
    return np.asarray(x).astype(np.float64)


def striped8(idx):
    return np.concatenate([x.reshape(-1, 16).T for x in idx]).astype(np.uint16)


def runs(offs, k):
    lists = np.stack([offs[16 * r : 16 * r + 16].T.reshape(-1) for r in range(8)]).astype(np.int64)
    return lists[np.arange(k) % 512 // 64]


def pack_weight(w):
    k, n = w.shape
    w = f64(np.asarray(w, np.float32).astype(ml_dtypes.bfloat16)).reshape(k // 32, 32, n)
    amax = np.abs(w).max(1)
    byte = np.clip(np.where(amax > 0, np.frexp(amax)[1] - 1 + 127 - 7, 1), 1, 254)
    scaled = (w * np.exp2(127.0 - byte)[:, None, :]).reshape(k, n).astype(np.float32)
    words = np.ascontiguousarray(scaled.reshape(k // 512, 128, 4, n).transpose(0, 1, 3, 2)).astype(ml_dtypes.float8_e4m3fn).view(np.uint8)
    return words, np.ascontiguousarray(byte.astype(np.uint8).reshape(k // 512, 16, n))


def unpack_weight(words, scales):
    g, p, n, _ = words.shape
    vals = np.ascontiguousarray(words).view(ml_dtypes.float8_e4m3fn).astype(np.float64) * np.repeat(np.exp2(scales.astype(np.float64) - 127.0), 8, axis=1)[..., None]
    return vals.transpose(0, 1, 3, 2).reshape(g * 512, n)

def planes(y):
    n, m = y.shape
    v = y.astype(np.float32).astype(ml_dtypes.bfloat16).astype(np.float64).reshape(n // 32, 32, m)
    top = np.abs(v).max(1)
    byte = np.clip(np.where(top > 0, np.frexp(top)[1] - 1 + 127 - 7, 1), 1, 254)
    codes = (v * np.exp2(127.0 - byte)[:, None, :]).reshape(n, m).astype(np.float32).astype(ml_dtypes.float8_e4m3fn).view(np.uint8)
    words = codes.reshape(n // 512, 128, 4, m).transpose(0, 1, 3, 2)
    return np.ascontiguousarray(words), np.ascontiguousarray(byte.astype(np.uint8).reshape(n // 512, 16, m))


K, T, S, N, H = 512, 2048, 512, 512, 512


def setup_inputs():
    n = np.random.standard_normal
    s = mx_kscale(K)[:, None]
    u = mx_kscale(S)
    packed_xT = pack_weight(n((K, T)) * s)
    return {
        "x_words": packed_xT[0],
        "x_scales": packed_xT[1],
        "wa": (n((K, H)) / np.sqrt(K) / s).astype(np.float32),
        "wb": (n((K, N)) / np.sqrt(K) / s).astype(np.float32),
        "gt": (np.random.uniform(0.5, 1.5, (S, 1)) * u[:, None]).astype(np.float32),
        "gi": (np.random.uniform(0.5, 1.5, (S, 1)) / u[:, None]).astype(np.float32),
        "offs": striped8(np.stack([np.random.permutation(T)[:S] for _ in range(8)])),
    }


def reference(x_words, x_scales, wa, wb, gt, gi, offs):
    xq = unpack_weight(x_words, x_scales)[np.arange(K)[:, None], runs(offs, K)]
    a = xq.T @ mxq(f64(wa), 0, "e4m3")
    z = f64(gt) * np.exp(0.5 * a)
    b = xq.T @ mxq(f64(wb), 0, "e4m3")
    z2 = f64(gi) * b
    out_0 = 0.03125 * ((mxq(z, 0, "e4m3").T @ mxq(z2, 0, "e4m3")))
    return (out_0,) + planes(out_0)

@@ -1,0 +1,158 @@
+from contextlib import ExitStack
+
+import concourse.mybir as mybir
+
+K, T, S, H, N = 512, 2048, 512, 512, 512
+FLOPS = 2 * K * S * H + 2 * K * S * N + 2 * S * H * N
+
+F32 = mybir.dt.float32
+BF16 = mybir.dt.bfloat16
+I32 = mybir.dt.int32
+U32 = mybir.dt.uint32
+U16 = mybir.dt.uint16
+U8 = mybir.dt.uint8
+FP8X4 = mybir.dt.float8_e4m3fn_x4
+ACT = mybir.ActivationFunctionType
+ALU = mybir.AluOpType
+
+P = 128
+PACK = 4
+CH = 128
+OUT_SCALE = 0.03125
+
+
+def tile_picked_expool_exp_po_kernel(tc, x_words, x_scales, wa, wb, gt, gi, offs, out_0, out_1, out_2):
+    nc = tc.nc
+    with ExitStack() as ctx:
+        keep = ctx.enter_context(tc.tile_pool(name="keep", bufs=1))
+        psum = ctx.enter_context(tc.psum_pool(name="psum", bufs=8))
+
+        def sb(name, shape, dtype):
+            return keep.tile(shape, dtype, name=name, align_bytes=64)
+
+        offsets = keep.tile([P, S // 16], U16, name="offsets")
+        nc.sync.dma_start(offsets[:], offs)
+
+        table_scales = sb("table_scales", [P, T], U8)
+        nc.sync.dma_start(table_scales[:].bitcast(I32), x_scales[0].bitcast(I32).unsqueeze(1).to_broadcast([16, 8, T // 4]))
+
+        gt_sb = sb("gt_sb", [P, PACK], F32)
+        gi_sb = sb("gi_sb", [P, PACK], F32)
+        nc.scalar.dma_start(gt_sb[:], gt.rearrange("(p t) o -> p (t o)", t=PACK))
+        nc.scalar.dma_start(gi_sb[:], gi.rearrange("(p t) o -> p (t o)", t=PACK))
+
+        table_words = sb("table_words", [P, T], U32)
+        nc.sync.dma_start(table_words[:].bitcast(I32), x_words[0].rearrange("p n t -> p (n t)").bitcast(I32))
+
+        def chunk_of(w, c):
+            return w.rearrange("(p j) n -> p j n", j=PACK)[:, :, c * CH : (c + 1) * CH]
+
+        raw = {}
+        for c in range(4):
+            raw["a", c] = sb("raw_a%d" % c, [P, PACK, CH], F32)[:]
+            nc.sync.dma_start(raw["a", c], chunk_of(wa, c))
+
+        warm = sb("warm", [P, 1], F32)
+        nc.scalar.activation(warm[:], gt_sb[:, 0:1], ACT.Exp, scale=0.0)
+
+        picked_scales = keep.tile([P, S], U8, name="picked_scales", tag="late", align_bytes=64)
+        nc.vector.tensor_copy(picked_scales[:], table_scales[:].indirect(offsets[:]))
+        x_sc = sb("x_sc", [P, S], U8)
+        nc.vector.tensor_copy(x_sc[:].rearrange("p (t m) -> p m t", t=PACK), picked_scales[:].rearrange("p (m t) -> p m t", t=PACK))
+        for j in range(1, 4):
+            nc.sync.dma_start(x_sc[j:P:32, :].bitcast(I32), x_sc[8 * j : P : 32, :].bitcast(I32))
+
+        late = keep.tile([P, 4, PACK, CH], F32, name="late", tag="late", align_bytes=64)
+        for c in range(4):
+            raw["b", c] = late[:, c]
+            nc.sync.dma_start(late[:, c], chunk_of(wb, c))
+
+        picked_words = sb("picked_words", [P, S], U32)
+        nc.vector.tensor_copy(picked_words[:], table_words[:].indirect(offsets[:]))
+        x_codes = sb("x_codes", [P, S], U32)
+        nc.vector.tensor_copy(x_codes[:].rearrange("p (t m) -> p m t", t=PACK), picked_words[:].rearrange("p (m t) -> p m t", t=PACK))
+
+        def quantise(name, values, width):
+            codes = sb(name + "_codes", [P, width], U32)
+            scales = sb(name + "_scales", [P, width], U8)
+            nc.vector.quantize_mx(out=codes[:].bitcast(FP8X4), scales=scales[:], in_=values)
+            return codes, scales
+
+        def interleave(engine, dst, src):
+            dst_v = dst.rearrange("p (c i) j -> p c j i", i=4)
+            src_v = src.rearrange("p j (c i) -> p c j i", i=4)
+            if engine == "S":
+                nc.scalar.copy(dst_v, src_v)
+            else:
+                nc.vector.tensor_copy(dst_v, src_v)
+
+        def four_products(lhs, rhs, cols):
+            bank = psum.tile([P, PACK, CH], F32, name="bank")
+            for t in range(PACK):
+                nc.tensor.matmul_mx(
+                    out=bank[:, t, :],
+                    lhsT=lhs[0][:, t * P : (t + 1) * P].bitcast(FP8X4),
+                    lhsT_scale=lhs[1][:, t * P : (t + 1) * P],
+                    rhs=rhs[0][:, cols].bitcast(FP8X4),
+                    rhs_scale=rhs[1][:, cols],
+                    start=True,
+                    stop=True,
+                )
+            return bank
+
+        x_op = (x_codes, x_sc)
+        z_bf = sb("z_bf", [P, PACK, P, PACK], BF16)
+        for c in range(4):
+            w_bf = sb("wa_bf%d" % c, [P, CH, PACK], BF16)
+            interleave("SSSV"[c], w_bf[:], raw["a", c])
+            w_op = quantise("wa%d" % c, w_bf[:].rearrange("p n j -> p (n j)"), CH)
+            bank = four_products(x_op, w_op, slice(0, CH))
+            e_sb = sb("e%d" % c, [P, PACK, CH // PACK, PACK], F32)
+            nc.scalar.activation(e_sb[:], bank[:].rearrange("p t (m u) -> p u m t", u=PACK), ACT.Exp, scale=0.5)
+            m0 = c * (CH // PACK)
+            nc.vector.tensor_tensor(
+                z_bf[:, :, m0 : m0 + CH // PACK, :],
+                e_sb[:],
+                gt_sb[:].unsqueeze(1).unsqueeze(1).to_broadcast([P, PACK, CH // PACK, PACK]),
+                ALU.mult,
+            )
+        z_op = quantise("z", z_bf[:].rearrange("p u m t -> p (u m t)"), H)
+
+        out_codes = sb("out_codes", [P, N], U32)
+        out_scales = sb("out_scales", [P, N], U8)
+        out_rows = out_0.rearrange("(p u) n -> p u n", u=PACK)
+        words_dram = out_1[0].rearrange("p n t -> p (n t)").bitcast(I32)
+        wb_ops = []
+        for c in range(4):
+            w_bf = sb("wb_bf%d" % c, [P, CH, PACK], BF16)
+            interleave("VVSS"[c], w_bf[:], raw["b", c])
+            wb_ops.append(quantise("wb%d" % c, w_bf[:].rearrange("p n j -> p (n j)"), CH))
+        z2_ops = []
+        for c in range(4):
+            bank = four_products(x_op, wb_ops[c], slice(0, CH))
+            z2_bf = sb("z2_bf%d" % c, [P, CH, PACK], BF16)
+            nc.vector.tensor_tensor(
+                z2_bf[:],
+                bank[:].rearrange("p t n -> p n t"),
+                gi_sb[:].unsqueeze(1).to_broadcast([P, CH, PACK]),
+                ALU.mult,
+            )
+            z2_ops.append(quantise("z2%d" % c, z2_bf[:].rearrange("p n t -> p (n t)"), CH))
+        for c in range(4):
+            cols = slice(c * CH, (c + 1) * CH)
+            bank = four_products(z_op, z2_ops[c], slice(0, CH))
+            y = sb("y%d" % c, [P, PACK, CH], F32)
+            nc.scalar.activation(y[:], bank[:], ACT.Copy, scale=OUT_SCALE)
+            nc.sync.dma_start(out_rows[:, :, cols], y[:])
+            y_bf = sb("y_bf%d" % c, [P, CH, PACK], BF16)
+            if c < 1:
+                nc.scalar.activation(y_bf[:], bank[:].rearrange("p u n -> p n u"), ACT.Copy, scale=OUT_SCALE)
+            else:
+                interleave("V", y_bf[:], y[:])
+            nc.vector.quantize_mx(out=out_codes[:, cols].bitcast(FP8X4), scales=out_scales[:, cols], in_=y_bf[:].rearrange("p n u -> p (n u)"))
+            if c % 2 == 1:
+                half = slice((c - 1) * CH, (c + 1) * CH)
+                nc.sync.dma_start(words_dram[:, half], out_codes[:, half].bitcast(I32))
+        for q in range(4):
+            engine = nc.sync if q % 2 == 0 else nc.scalar
+            engine.dma_start(out_2[0, 4 * q : 4 * q + 4, :].bitcast(I32), out_scales[32 * q : 32 * q + 4, :].bitcast(I32))

@@ -18,7 +18,15 @@ ALU = mybir.AluOpType
 P = 128
 PACK = 4
 CH = 128
+HALF = 256
 OUT_SCALE = 0.03125
+CAST_A = "SVVV"
+CAST_B = "VSVS"
+Z2 = "VSVS"
+YENG = "SSSV"
+YBF = "VVVV"
+LOADS = ["a0123","b01","b2","b3"]
+HOLD = 2
 
 
 def tile_picked_expool_exp_po_kernel(tc, x_words, x_scales, wa, wb, gt, gi, offs, out_0, out_1, out_2):
@@ -26,6 +34,7 @@ def tile_picked_expool_exp_po_kernel(tc, x_words, x_scales, wa, wb, gt, gi, offs
     with ExitStack() as ctx:
         keep = ctx.enter_context(tc.tile_pool(name="keep", bufs=1))
         psum = ctx.enter_context(tc.psum_pool(name="psum", bufs=8))
+        queue = {"Q": nc.sync, "S": nc.scalar}
 
         def sb(name, shape, dtype):
             return keep.tile(shape, dtype, name=name, align_bytes=64)
@@ -34,23 +43,31 @@ def tile_picked_expool_exp_po_kernel(tc, x_words, x_scales, wa, wb, gt, gi, offs
         nc.sync.dma_start(offsets[:], offs)
 
         table_scales = sb("table_scales", [P, T], U8)
-        nc.sync.dma_start(table_scales[:].bitcast(I32), x_scales[0].bitcast(I32).unsqueeze(1).to_broadcast([16, 8, T // 4]))
+        nc.vector.memset(table_scales[:].bitcast(I32), 0)
+        table_words = sb("table_words", [P, T], U32)
+        words_in = x_words[0].rearrange("p n t -> p (n t)").bitcast(I32)
+        nc.sync.dma_start(table_words[:, 0 : T // 4].bitcast(I32), words_in[:, 0 : T // 4])
+        for e in range(2):
+            nc.sync.dma_start(table_scales[e:P:16, :].bitcast(I32), x_scales[0, e:16:2, :].bitcast(I32))
 
         gt_sb = sb("gt_sb", [P, PACK], F32)
         gi_sb = sb("gi_sb", [P, PACK], F32)
         nc.scalar.dma_start(gt_sb[:], gt.rearrange("(p t) o -> p (t o)", t=PACK))
         nc.scalar.dma_start(gi_sb[:], gi.rearrange("(p t) o -> p (t o)", t=PACK))
 
-        table_words = sb("table_words", [P, T], U32)
-        nc.sync.dma_start(table_words[:].bitcast(I32), x_words[0].rearrange("p n t -> p (n t)").bitcast(I32))
-
-        def chunk_of(w, c):
-            return w.rearrange("(p j) n -> p j n", j=PACK)[:, :, c * CH : (c + 1) * CH]
+        nc.sync.dma_start(table_words[:, T // 4 : T].bitcast(I32), words_in[:, T // 4 : T])
 
         raw = {}
-        for c in range(4):
-            raw["a", c] = sb("raw_a%d" % c, [P, PACK, CH], F32)[:]
-            nc.sync.dma_start(raw["a", c], chunk_of(wa, c))
+
+        def load(group, dst):
+            w = {"a": wa, "b": wb}[group[0]]
+            first, count = int(group[1]), len(group) - 1
+            nc.sync.dma_start(dst, w.rearrange("(p j) n -> p j n", j=PACK)[:, :, first * CH : (first + count) * CH])
+            for i in range(count):
+                raw[group[0], first + i] = dst[:, :, i * CH : (i + 1) * CH]
+
+        for group in LOADS[:HOLD]:
+            load(group, sb("raw_" + group, [P, PACK, (len(group) - 1) * CH], F32)[:])
 
         warm = sb("warm", [P, 1], F32)
         nc.scalar.activation(warm[:], gt_sb[:, 0:1], ACT.Exp, scale=0.0)
@@ -59,24 +76,27 @@ def tile_picked_expool_exp_po_kernel(tc, x_words, x_scales, wa, wb, gt, gi, offs
         nc.vector.tensor_copy(picked_scales[:], table_scales[:].indirect(offsets[:]))
         x_sc = sb("x_sc", [P, S], U8)
         nc.vector.tensor_copy(x_sc[:].rearrange("p (t m) -> p m t", t=PACK), picked_scales[:].rearrange("p (m t) -> p m t", t=PACK))
-        for j in range(1, 4):
-            nc.sync.dma_start(x_sc[j:P:32, :].bitcast(I32), x_sc[8 * j : P : 32, :].bitcast(I32))
+        for e in range(2):
+            queue["S"].dma_start(x_sc[2 + e : P : 32, :].bitcast(I32), x_sc[16 + e : P : 32, :].bitcast(I32))
 
-        late = keep.tile([P, 4, PACK, CH], F32, name="late", tag="late", align_bytes=64)
-        for c in range(4):
-            raw["b", c] = late[:, c]
-            nc.sync.dma_start(late[:, c], chunk_of(wb, c))
+        late_chunks = sum(len(group) - 1 for group in LOADS[HOLD:])
+        late = keep.tile([P, late_chunks * PACK * CH], F32, name="late", tag="late", align_bytes=64)
+        at = 0
+        for group in LOADS[HOLD:]:
+            size = (len(group) - 1) * PACK * CH
+            load(group, late[:, at : at + size].rearrange("p (j n) -> p j n", j=PACK))
+            at = at + size
 
         picked_words = sb("picked_words", [P, S], U32)
         nc.vector.tensor_copy(picked_words[:], table_words[:].indirect(offsets[:]))
         x_codes = sb("x_codes", [P, S], U32)
         nc.vector.tensor_copy(x_codes[:].rearrange("p (t m) -> p m t", t=PACK), picked_words[:].rearrange("p (m t) -> p m t", t=PACK))
 
-        def quantise(name, values, width):
-            codes = sb(name + "_codes", [P, width], U32)
-            scales = sb(name + "_scales", [P, width], U8)
-            nc.vector.quantize_mx(out=codes[:].bitcast(FP8X4), scales=scales[:], in_=values)
-            return codes, scales
+        def operand(name, width):
+            return sb(name + "_codes", [P, width], U32), sb(name + "_scales", [P, width], U8)
+
+        def quantise(op, cols, values):
+            nc.vector.quantize_mx(out=op[0][:, cols].bitcast(FP8X4), scales=op[1][:, cols], in_=values)
 
         def interleave(engine, dst, src):
             dst_v = dst.rearrange("p (c i) j -> p c j i", i=4)
@@ -86,27 +106,31 @@ def tile_picked_expool_exp_po_kernel(tc, x_words, x_scales, wa, wb, gt, gi, offs
             else:
                 nc.vector.tensor_copy(dst_v, src_v)
 
-        def four_products(lhs, rhs, cols):
-            bank = psum.tile([P, PACK, CH], F32, name="bank")
-            for t in range(PACK):
+        def products(lhs, tiles, rhs, width):
+            bank = psum.tile([P, len(tiles), width], F32, name="bank")
+            for i, t in enumerate(tiles):
                 nc.tensor.matmul_mx(
-                    out=bank[:, t, :],
+                    out=bank[:, i, :],
                     lhsT=lhs[0][:, t * P : (t + 1) * P].bitcast(FP8X4),
                     lhsT_scale=lhs[1][:, t * P : (t + 1) * P],
-                    rhs=rhs[0][:, cols].bitcast(FP8X4),
-                    rhs_scale=rhs[1][:, cols],
+                    rhs=rhs[0][:].bitcast(FP8X4),
+                    rhs_scale=rhs[1][:],
                     start=True,
                     stop=True,
                 )
             return bank
 
+        def weights(name, c, engine):
+            w_bf = sb("w%s_bf%d" % (name, c), [P, CH, PACK], BF16)
+            interleave(engine, w_bf[:], raw[name, c])
+            op = operand("w%s%d" % (name, c), CH)
+            quantise(op, slice(0, CH), w_bf[:].rearrange("p n j -> p (n j)"))
+            return op
+
         x_op = (x_codes, x_sc)
         z_bf = sb("z_bf", [P, PACK, P, PACK], BF16)
         for c in range(4):
-            w_bf = sb("wa_bf%d" % c, [P, CH, PACK], BF16)
-            interleave("SSSV"[c], w_bf[:], raw["a", c])
-            w_op = quantise("wa%d" % c, w_bf[:].rearrange("p n j -> p (n j)"), CH)
-            bank = four_products(x_op, w_op, slice(0, CH))
+            bank = products(x_op, range(PACK), weights("a", c, CAST_A[c]), CH)
             e_sb = sb("e%d" % c, [P, PACK, CH // PACK, PACK], F32)
             nc.scalar.activation(e_sb[:], bank[:].rearrange("p t (m u) -> p u m t", u=PACK), ACT.Exp, scale=0.5)
             m0 = c * (CH // PACK)
@@ -116,43 +140,53 @@ def tile_picked_expool_exp_po_kernel(tc, x_words, x_scales, wa, wb, gt, gi, offs
                 gt_sb[:].unsqueeze(1).unsqueeze(1).to_broadcast([P, PACK, CH // PACK, PACK]),
                 ALU.mult,
             )
-        z_op = quantise("z", z_bf[:].rearrange("p u m t -> p (u m t)"), H)
 
-        out_codes = sb("out_codes", [P, N], U32)
-        out_scales = sb("out_scales", [P, N], U8)
-        out_rows = out_0.rearrange("(p u) n -> p u n", u=PACK)
-        words_dram = out_1[0].rearrange("p n t -> p (n t)").bitcast(I32)
-        wb_ops = []
-        for c in range(4):
-            w_bf = sb("wb_bf%d" % c, [P, CH, PACK], BF16)
-            interleave("VVSS"[c], w_bf[:], raw["b", c])
-            wb_ops.append(quantise("wb%d" % c, w_bf[:].rearrange("p n j -> p (n j)"), CH))
-        z2_ops = []
-        for c in range(4):
-            bank = four_products(x_op, wb_ops[c], slice(0, CH))
+        wb_ops = [weights("b", c, CAST_B[c]) for c in range(4)]
+        z2_ops = [operand("z2_%d" % h, HALF) for h in range(2)]
+
+        def values(c):
+            bank = products(x_op, range(PACK), wb_ops[c], CH)
             z2_bf = sb("z2_bf%d" % c, [P, CH, PACK], BF16)
-            nc.vector.tensor_tensor(
-                z2_bf[:],
-                bank[:].rearrange("p t n -> p n t"),
-                gi_sb[:].unsqueeze(1).to_broadcast([P, CH, PACK]),
-                ALU.mult,
-            )
-            z2_ops.append(quantise("z2%d" % c, z2_bf[:].rearrange("p n t -> p (n t)"), CH))
-        for c in range(4):
-            cols = slice(c * CH, (c + 1) * CH)
-            bank = four_products(z_op, z2_ops[c], slice(0, CH))
-            y = sb("y%d" % c, [P, PACK, CH], F32)
-            nc.scalar.activation(y[:], bank[:], ACT.Copy, scale=OUT_SCALE)
-            nc.sync.dma_start(out_rows[:, :, cols], y[:])
-            y_bf = sb("y_bf%d" % c, [P, CH, PACK], BF16)
-            if c < 1:
-                nc.scalar.activation(y_bf[:], bank[:].rearrange("p u n -> p n u"), ACT.Copy, scale=OUT_SCALE)
+            if Z2[c] == "V":
+                nc.vector.tensor_tensor(
+                    z2_bf[:],
+                    bank[:].rearrange("p t n -> p n t"),
+                    gi_sb[:].unsqueeze(1).to_broadcast([P, CH, PACK]),
+                    ALU.mult,
+                )
             else:
-                interleave("V", y_bf[:], y[:])
-            nc.vector.quantize_mx(out=out_codes[:, cols].bitcast(FP8X4), scales=out_scales[:, cols], in_=y_bf[:].rearrange("p n u -> p (n u)"))
-            if c % 2 == 1:
-                half = slice((c - 1) * CH, (c + 1) * CH)
-                nc.sync.dma_start(words_dram[:, half], out_codes[:, half].bitcast(I32))
+                rows = sb("z2_rows%d" % c, [P, PACK, CH], BF16)
+                for t in range(PACK):
+                    nc.scalar.activation(rows[:, t, :], bank[:, t, :], ACT.Copy, scale=gi_sb[:, t : t + 1])
+                interleave("V", z2_bf[:], rows[:])
+            quantise(z2_ops[c // 2], slice((c % 2) * CH, (c % 2 + 1) * CH), z2_bf[:].rearrange("p n t -> p (n t)"))
+
+        values(0)
+        values(1)
+        z_op = operand("z", H)
+        for g in range(2):
+            quantise(z_op, slice(g * HALF, (g + 1) * HALF), z_bf[:, 2 * g : 2 * g + 2].rearrange("p u m t -> p (u m t)"))
+        values(2)
+        values(3)
+
+        out_op = operand("out", N)
+        out_rows = out_0.rearrange("(p u) n -> p u n", u=PACK)
+        words_out = out_1[0].rearrange("p n t -> p (n t)").bitcast(I32)
+        for h in range(2):
+            half = slice(h * HALF, (h + 1) * HALF)
+            y = sb("y%d" % h, [P, PACK, HALF], F32)
+            for g in range(2):
+                pair = slice(2 * g, 2 * g + 2)
+                bank = products(z_op, range(2 * g, 2 * g + 2), z2_ops[h], HALF)
+                if YENG[2 * h + g] == "S":
+                    nc.scalar.activation(y[:, pair, :], bank[:], ACT.Copy, scale=OUT_SCALE)
+                else:
+                    nc.vector.tensor_scalar(y[:, pair, :], bank[:], OUT_SCALE, None, ALU.mult)
+                queue["QSQS"[2 * h + g]].dma_start(out_rows[:, pair, half], y[:, pair, :])
+            for c in range(2 * h, 2 * h + 2):
+                y_bf = sb("y_bf%d" % c, [P, CH, PACK], BF16)
+                interleave(YBF[c], y_bf[:], y[:, :, (c % 2) * CH : (c % 2 + 1) * CH])
+                quantise(out_op, slice(c * CH, (c + 1) * CH), y_bf[:].rearrange("p n u -> p (n u)"))
+            queue["SS"[h]].dma_start(words_out[:, half], out_op[0][:, half].bitcast(I32))
         for q in range(4):
-            engine = nc.sync if q % 2 == 0 else nc.scalar
-            engine.dma_start(out_2[0, 4 * q : 4 * q + 4, :].bitcast(I32), out_scales[32 * q : 32 * q + 4, :].bitcast(I32))
+            queue["QQQQ"[q]].dma_start(out_2[0, 4 * q : 4 * q + 4, :].bitcast(I32), out_op[1][32 * q : 32 * q + 4, :].bitcast(I32))

@@ -1,6 +1,7 @@
 from contextlib import ExitStack
 
 import concourse.mybir as mybir
+from concourse.masks import make_identity
 
 K, T, S, H, N = 512, 2048, 512, 512, 512
 FLOPS = 2 * K * S * H + 2 * K * S * N + 2 * S * H * N
@@ -20,12 +21,12 @@ PACK = 4
 CH = 128
 HALF = 256
 OUT_SCALE = 0.03125
-CAST_A = "SVVV"
-CAST_B = "VSVS"
-Z2 = "VSVS"
+CAST_A = "SSVV"
+CAST_B = "VSSS"
+Z2 = "VVVV"
 YENG = "SSSV"
 YBF = "VVVV"
-LOADS = ["a0123","b01","b2","b3"]
+LOADS = ["a01","a23","b0","b1","b23"]
 HOLD = 2
 
 
@@ -50,10 +51,9 @@ def tile_picked_expool_exp_po_kernel(tc, x_words, x_scales, wa, wb, gt, gi, offs
         for e in range(2):
             nc.sync.dma_start(table_scales[e:P:16, :].bitcast(I32), x_scales[0, e:16:2, :].bitcast(I32))
 
-        gt_sb = sb("gt_sb", [P, PACK], F32)
-        gi_sb = sb("gi_sb", [P, PACK], F32)
-        nc.scalar.dma_start(gt_sb[:], gt.rearrange("(p t) o -> p (t o)", t=PACK))
-        nc.scalar.dma_start(gi_sb[:], gi.rearrange("(p t) o -> p (t o)", t=PACK))
+        gates = sb("gates", [P, 2, 32], F32)
+        for i, gate in enumerate((gt, gi)):
+            nc.scalar.dma_start(gates[:, i, :], gate.rearrange("(b k) o -> b (k o)", k=32).unsqueeze(1).to_broadcast([16, 8, 32]))
 
         nc.sync.dma_start(table_words[:, T // 4 : T].bitcast(I32), words_in[:, T // 4 : T])
 
@@ -70,14 +70,30 @@ def tile_picked_expool_exp_po_kernel(tc, x_words, x_scales, wa, wb, gt, gi, offs
             load(group, sb("raw_" + group, [P, PACK, (len(group) - 1) * CH], F32)[:])
 
         warm = sb("warm", [P, 1], F32)
-        nc.scalar.activation(warm[:], gt_sb[:, 0:1], ACT.Exp, scale=0.0)
+        nc.scalar.activation(warm[:], gates[:, 0, 0:1], ACT.Exp, scale=0.0)
+
+        identity = sb("identity", [P, P], F32)
+        make_identity(nc, identity[:])
+        own = sb("own", [P, 8], F32)
+        nc.vector.tensor_reduce(own[:], identity[:].rearrange("p (b r) -> p r b", r=8), mybir.AxisListType.X, ALU.add)
+        masked = sb("masked", [P, 2 * PACK, 8], F32)
+        nc.vector.tensor_tensor(
+            masked[:], gates[:].rearrange("p s (t r) -> p (s t) r", r=8), own[:].unsqueeze(1).to_broadcast([P, 2 * PACK, 8]), ALU.mult
+        )
+        dealt = sb("dealt", [P, 2 * PACK], F32)
+        nc.vector.tensor_reduce(dealt[:], masked[:], mybir.AxisListType.X, ALU.add)
+        gt_sb = dealt[:, 0:PACK]
+        gi_sb = dealt[:, PACK : 2 * PACK]
 
         picked_scales = keep.tile([P, S], U8, name="picked_scales", tag="late", align_bytes=64)
         nc.vector.tensor_copy(picked_scales[:], table_scales[:].indirect(offsets[:]))
         x_sc = sb("x_sc", [P, S], U8)
-        nc.vector.tensor_copy(x_sc[:].rearrange("p (t m) -> p m t", t=PACK), picked_scales[:].rearrange("p (m t) -> p m t", t=PACK))
+        nc.vector.tensor_copy(
+            x_sc[:].bitcast(I32).rearrange("p (t b w) -> p t b w", t=PACK, w=2),
+            picked_scales[:].bitcast(I32).rearrange("p (b t w) -> p t b w", t=PACK, w=2),
+        )
         for e in range(2):
-            queue["S"].dma_start(x_sc[2 + e : P : 32, :].bitcast(I32), x_sc[16 + e : P : 32, :].bitcast(I32))
+            queue["Q"].dma_start(x_sc[2 + e : P : 32, :].bitcast(I32), x_sc[16 + e : P : 32, :].bitcast(I32))
 
         late_chunks = sum(len(group) - 1 for group in LOADS[HOLD:])
         late = keep.tile([P, late_chunks * PACK * CH], F32, name="late", tag="late", align_bytes=64)
@@ -90,7 +106,9 @@ def tile_picked_expool_exp_po_kernel(tc, x_words, x_scales, wa, wb, gt, gi, offs
         picked_words = sb("picked_words", [P, S], U32)
         nc.vector.tensor_copy(picked_words[:], table_words[:].indirect(offsets[:]))
         x_codes = sb("x_codes", [P, S], U32)
-        nc.vector.tensor_copy(x_codes[:].rearrange("p (t m) -> p m t", t=PACK), picked_words[:].rearrange("p (m t) -> p m t", t=PACK))
+        nc.vector.tensor_copy(
+            x_codes[:].rearrange("p (t b r) -> p t b r", t=PACK, r=8), picked_words[:].rearrange("p (b t r) -> p t b r", t=PACK, r=8)
+        )
 
         def operand(name, width):
             return sb(name + "_codes", [P, width], U32), sb(name + "_scales", [P, width], U8)
@@ -137,12 +155,12 @@ def tile_picked_expool_exp_po_kernel(tc, x_words, x_scales, wa, wb, gt, gi, offs
             nc.vector.tensor_tensor(
                 z_bf[:, :, m0 : m0 + CH // PACK, :],
                 e_sb[:],
-                gt_sb[:].unsqueeze(1).unsqueeze(1).to_broadcast([P, PACK, CH // PACK, PACK]),
+                gt_sb.unsqueeze(1).unsqueeze(1).to_broadcast([P, PACK, CH // PACK, PACK]),
                 ALU.mult,
             )
 
         wb_ops = [weights("b", c, CAST_B[c]) for c in range(4)]
-        z2_ops = [operand("z2_%d" % h, HALF) for h in range(2)]
+        z2_ops = [operand("z2_0", CH), operand("z2_1", CH), operand("z2_23", HALF)]
 
         def values(c):
             bank = products(x_op, range(PACK), wb_ops[c], CH)
@@ -151,7 +169,7 @@ def tile_picked_expool_exp_po_kernel(tc, x_words, x_scales, wa, wb, gt, gi, offs
                 nc.vector.tensor_tensor(
                     z2_bf[:],
                     bank[:].rearrange("p t n -> p n t"),
-                    gi_sb[:].unsqueeze(1).to_broadcast([P, CH, PACK]),
+                    gi_sb.unsqueeze(1).to_broadcast([P, CH, PACK]),
                     ALU.mult,
                 )
             else:
@@ -159,7 +177,8 @@ def tile_picked_expool_exp_po_kernel(tc, x_words, x_scales, wa, wb, gt, gi, offs
                 for t in range(PACK):
                     nc.scalar.activation(rows[:, t, :], bank[:, t, :], ACT.Copy, scale=gi_sb[:, t : t + 1])
                 interleave("V", z2_bf[:], rows[:])
-            quantise(z2_ops[c // 2], slice((c % 2) * CH, (c % 2 + 1) * CH), z2_bf[:].rearrange("p n t -> p (n t)"))
+            at = max(c - 2, 0) * CH
+            quantise(z2_ops[min(c, 2)], slice(at, at + CH), z2_bf[:].rearrange("p n t -> p (n t)"))
 
         values(0)
         values(1)
@@ -172,21 +191,31 @@ def tile_picked_expool_exp_po_kernel(tc, x_words, x_scales, wa, wb, gt, gi, offs
         out_op = operand("out", N)
         out_rows = out_0.rearrange("(p u) n -> p u n", u=PACK)
         words_out = out_1[0].rearrange("p n t -> p (n t)").bitcast(I32)
-        for h in range(2):
-            half = slice(h * HALF, (h + 1) * HALF)
-            y = sb("y%d" % h, [P, PACK, HALF], F32)
-            for g in range(2):
-                pair = slice(2 * g, 2 * g + 2)
-                bank = products(z_op, range(2 * g, 2 * g + 2), z2_ops[h], HALF)
-                if YENG[2 * h + g] == "S":
-                    nc.scalar.activation(y[:, pair, :], bank[:], ACT.Copy, scale=OUT_SCALE)
-                else:
-                    nc.vector.tensor_scalar(y[:, pair, :], bank[:], OUT_SCALE, None, ALU.mult)
-                queue["QSQS"[2 * h + g]].dma_start(out_rows[:, pair, half], y[:, pair, :])
-            for c in range(2 * h, 2 * h + 2):
-                y_bf = sb("y_bf%d" % c, [P, CH, PACK], BF16)
-                interleave(YBF[c], y_bf[:], y[:, :, (c % 2) * CH : (c % 2 + 1) * CH])
-                quantise(out_op, slice(c * CH, (c + 1) * CH), y_bf[:].rearrange("p n u -> p (n u)"))
-            queue["SS"[h]].dma_start(words_out[:, half], out_op[0][:, half].bitcast(I32))
+
+        def planes(c, y):
+            y_bf = sb("y_bf%d" % c, [P, CH, PACK], BF16)
+            interleave("V", y_bf[:], y)
+            quantise(out_op, slice(c * CH, (c + 1) * CH), y_bf[:].rearrange("p n u -> p (n u)"))
+            if c % 2 == 1:
+                half = slice((c - 1) * CH, (c + 1) * CH)
+                nc.sync.dma_start(words_out[:, half], out_op[0][:, half].bitcast(I32))
+
+        for c in range(2):
+            bank = products(z_op, range(PACK), z2_ops[c], CH)
+            y = sb("y%d" % c, [P, PACK, CH], F32)
+            nc.scalar.activation(y[:], bank[:], ACT.Copy, scale=OUT_SCALE)
+            nc.sync.dma_start(out_rows[:, :, c * CH : (c + 1) * CH], y[:])
+            planes(c, y[:])
+        y = sb("y23", [P, PACK, HALF], F32)
+        for g in range(2):
+            pair = slice(2 * g, 2 * g + 2)
+            bank = products(z_op, range(2 * g, 2 * g + 2), z2_ops[2], HALF)
+            if g == 0:
+                nc.scalar.activation(y[:, pair, :], bank[:], ACT.Copy, scale=OUT_SCALE)
+            else:
+                nc.vector.tensor_scalar(y[:, pair, :], bank[:], OUT_SCALE, None, ALU.mult)
+            nc.sync.dma_start(out_rows[:, pair, HALF:N], y[:, pair, :])
+        for c in range(2, 4):
+            planes(c, y[:, :, (c - 2) * CH : (c - 1) * CH])
         for q in range(4):
-            queue["QQQQ"[q]].dma_start(out_2[0, 4 * q : 4 * q + 4, :].bitcast(I32), out_op[1][32 * q : 32 * q + 4, :].bitcast(I32))
+            queue["QSQS"[q]].dma_start(out_2[0, 4 * q : 4 * q + 4, :].bitcast(I32), out_op[1][32 * q : 32 * q + 4, :].bitcast(I32))

@@ -22,12 +22,16 @@ CH = 128
 HALF = 256
 OUT_SCALE = 0.03125
 CAST_A = "SSVV"
-CAST_B = "VSSS"
-Z2 = "VVVV"
-YENG = "SSSV"
+CAST_B = "VVSS"
+Z2 = "VSSS"
+YENG = "SSSS"
 YBF = "VVVV"
-LOADS = ["a01","a23","b0","b1","b23"]
+LOADS = ["a01","a23","b01","b23"]
 HOLD = 2
+SEQ = ["pa0","pa1","pa2","pa3","pb0","pb1","pb2","pb3","A0","A1","A2","A3","Z","B0","B1","B2","B3","O0","O1","O2","O3"]
+WIDE = ""
+PAIRS = "y"
+QZ = 2
 
 
 def tile_picked_expool_exp_po_kernel(tc, x_words, x_scales, wa, wb, gt, gi, offs, out_0, out_1, out_2):
@@ -131,24 +135,46 @@ def tile_picked_expool_exp_po_kernel(tc, x_words, x_scales, wa, wb, gt, gi, offs
                     out=bank[:, i, :],
                     lhsT=lhs[0][:, t * P : (t + 1) * P].bitcast(FP8X4),
                     lhsT_scale=lhs[1][:, t * P : (t + 1) * P],
-                    rhs=rhs[0][:].bitcast(FP8X4),
-                    rhs_scale=rhs[1][:],
+                    rhs=rhs[0].bitcast(FP8X4),
+                    rhs_scale=rhs[1],
                     start=True,
                     stop=True,
                 )
             return bank
 
-        def weights(name, c, engine):
-            w_bf = sb("w%s_bf%d" % (name, c), [P, CH, PACK], BF16)
-            interleave(engine, w_bf[:], raw[name, c])
-            op = operand("w%s%d" % (name, c), CH)
-            quantise(op, slice(0, CH), w_bf[:].rearrange("p n j -> p (n j)"))
-            return op
+        w_ops = {}
+        w_bfs = {}
+
+        def weights(name, c):
+            engine = {"a": CAST_A, "b": CAST_B}[name][c]
+            if name in PAIRS:
+                if c % 2 == 0:
+                    w_bfs[name, c // 2] = sb("w%s_bf%d" % (name, c), [P, HALF, PACK], BF16)
+                w_bf = w_bfs[name, c // 2]
+                interleave(engine, w_bf[:, (c % 2) * CH : (c % 2 + 1) * CH, :], raw[name, c])
+                if c % 2 == 1:
+                    op = operand("w%s%d" % (name, c), HALF)
+                    quantise(op, slice(0, HALF), w_bf[:].rearrange("p n j -> p (n j)"))
+                    w_ops[name, c - 1] = (op[0][:, 0:CH], op[1][:, 0:CH])
+                    w_ops[name, c] = (op[0][:, CH:HALF], op[1][:, CH:HALF])
+            else:
+                w_bf = sb("w%s_bf%d" % (name, c), [P, CH, PACK], BF16)
+                interleave(engine, w_bf[:], raw[name, c])
+                op = operand("w%s%d" % (name, c), CH)
+                quantise(op, slice(0, CH), w_bf[:].rearrange("p n j -> p (n j)"))
+                w_ops[name, c] = (op[0][:], op[1][:])
 
         x_op = (x_codes, x_sc)
         z_bf = sb("z_bf", [P, PACK, P, PACK], BF16)
-        for c in range(4):
-            bank = products(x_op, range(PACK), weights("a", c, CAST_A[c]), CH)
+        z_op = operand("z", H)
+        z2_ops = [operand("z2_%d" % h, HALF) for h in range(2)]
+        out_op = operand("out", N)
+        out_rows = out_0.rearrange("(p u) n -> p u n", u=PACK)
+        words_out = out_1[0].rearrange("p n t -> p (n t)").bitcast(I32)
+        y_bfs = {}
+
+        def scores(c):
+            bank = products(x_op, range(PACK), w_ops["a", c], CH)
             e_sb = sb("e%d" % c, [P, PACK, CH // PACK, PACK], F32)
             nc.scalar.activation(e_sb[:], bank[:].rearrange("p t (m u) -> p u m t", u=PACK), ACT.Exp, scale=0.5)
             m0 = c * (CH // PACK)
@@ -159,11 +185,13 @@ def tile_picked_expool_exp_po_kernel(tc, x_words, x_scales, wa, wb, gt, gi, offs
                 ALU.mult,
             )
 
-        wb_ops = [weights("b", c, CAST_B[c]) for c in range(4)]
-        z2_ops = [operand("z2_0", CH), operand("z2_1", CH), operand("z2_23", HALF)]
+        def quantise_z():
+            n = PACK // QZ
+            for g in range(QZ):
+                quantise(z_op, slice(g * n * P, (g + 1) * n * P), z_bf[:, n * g : n * g + n].rearrange("p u m t -> p (u m t)"))
 
         def values(c):
-            bank = products(x_op, range(PACK), wb_ops[c], CH)
+            bank = products(x_op, range(PACK), w_ops["b", c], CH)
             z2_bf = sb("z2_bf%d" % c, [P, CH, PACK], BF16)
             if Z2[c] == "V":
                 nc.vector.tensor_tensor(
@@ -177,45 +205,65 @@ def tile_picked_expool_exp_po_kernel(tc, x_words, x_scales, wa, wb, gt, gi, offs
                 for t in range(PACK):
                     nc.scalar.activation(rows[:, t, :], bank[:, t, :], ACT.Copy, scale=gi_sb[:, t : t + 1])
                 interleave("V", z2_bf[:], rows[:])
-            at = max(c - 2, 0) * CH
-            quantise(z2_ops[min(c, 2)], slice(at, at + CH), z2_bf[:].rearrange("p n t -> p (n t)"))
+            quantise(z2_ops[c // 2], slice((c % 2) * CH, (c % 2 + 1) * CH), z2_bf[:].rearrange("p n t -> p (n t)"))
 
-        values(0)
-        values(1)
-        z_op = operand("z", H)
-        for g in range(2):
-            quantise(z_op, slice(g * HALF, (g + 1) * HALF), z_bf[:, 2 * g : 2 * g + 2].rearrange("p u m t -> p (u m t)"))
-        values(2)
-        values(3)
-
-        out_op = operand("out", N)
-        out_rows = out_0.rearrange("(p u) n -> p u n", u=PACK)
-        words_out = out_1[0].rearrange("p n t -> p (n t)").bitcast(I32)
-
-        def planes(c, y):
-            y_bf = sb("y_bf%d" % c, [P, CH, PACK], BF16)
-            interleave("V", y_bf[:], y)
-            quantise(out_op, slice(c * CH, (c + 1) * CH), y_bf[:].rearrange("p n u -> p (n u)"))
-            if c % 2 == 1:
-                half = slice((c - 1) * CH, (c + 1) * CH)
-                nc.sync.dma_start(words_out[:, half], out_op[0][:, half].bitcast(I32))
-
-        for c in range(2):
-            bank = products(z_op, range(PACK), z2_ops[c], CH)
-            y = sb("y%d" % c, [P, PACK, CH], F32)
-            nc.scalar.activation(y[:], bank[:], ACT.Copy, scale=OUT_SCALE)
-            nc.sync.dma_start(out_rows[:, :, c * CH : (c + 1) * CH], y[:])
-            planes(c, y[:])
-        y = sb("y23", [P, PACK, HALF], F32)
-        for g in range(2):
-            pair = slice(2 * g, 2 * g + 2)
-            bank = products(z_op, range(2 * g, 2 * g + 2), z2_ops[2], HALF)
-            if g == 0:
-                nc.scalar.activation(y[:, pair, :], bank[:], ACT.Copy, scale=OUT_SCALE)
+        def scaled(engine, dst, src):
+            if engine == "S":
+                nc.scalar.activation(dst, src, ACT.Copy, scale=OUT_SCALE)
             else:
-                nc.vector.tensor_scalar(y[:, pair, :], bank[:], OUT_SCALE, None, ALU.mult)
-            nc.sync.dma_start(out_rows[:, pair, HALF:N], y[:, pair, :])
-        for c in range(2, 4):
-            planes(c, y[:, :, (c - 2) * CH : (c - 1) * CH])
+                nc.vector.tensor_scalar(dst, src, OUT_SCALE, None, ALU.mult)
+
+        def planes(c, y, bank):
+            h = c // 2
+            half = slice(h * HALF, (h + 1) * HALF)
+            if "y" in PAIRS:
+                if c % 2 == 0:
+                    y_bfs[h] = sb("y_bf%d" % c, [P, HALF, PACK], BF16)
+                dst = y_bfs[h][:, (c % 2) * CH : (c % 2 + 1) * CH, :]
+            else:
+                dst = sb("y_bf%d" % c, [P, CH, PACK], BF16)[:]
+            if YBF[c] == "S" and bank is not None:
+                scaled("S", dst, bank[:].rearrange("p u n -> p n u"))
+            else:
+                interleave(YBF[c], dst, y)
+            if "y" not in PAIRS:
+                quantise(out_op, slice(c * CH, (c + 1) * CH), dst.rearrange("p n u -> p (n u)"))
+            elif c % 2 == 1:
+                quantise(out_op, half, y_bfs[h][:].rearrange("p n u -> p (n u)"))
+            if c % 2 == 1:
+                queue["SS"[h]].dma_start(words_out[:, half], out_op[0][:, half].bitcast(I32))
+
+        def output(c):
+            h = c // 2
+            if str(h) in WIDE:
+                if c % 2 == 0:
+                    return
+                y = sb("y%d" % c, [P, PACK, HALF], F32)
+                for g in range(2):
+                    pair = slice(2 * g, 2 * g + 2)
+                    bank = products(z_op, range(2 * g, 2 * g + 2), (z2_ops[h][0][:], z2_ops[h][1][:]), HALF)
+                    scaled(YENG[2 * h + g], y[:, pair, :], bank[:])
+                    queue["QQQQ"[2 * h + g]].dma_start(out_rows[:, pair, h * HALF : (h + 1) * HALF], y[:, pair, :])
+                for k in range(2):
+                    planes(2 * h + k, y[:, :, k * CH : (k + 1) * CH], None)
+            else:
+                cols = slice((c % 2) * CH, (c % 2 + 1) * CH)
+                bank = products(z_op, range(PACK), (z2_ops[h][0][:, cols], z2_ops[h][1][:, cols]), CH)
+                y = sb("y%d" % c, [P, PACK, CH], F32)
+                scaled(YENG[c], y[:], bank[:])
+                queue["QQQQ"[c]].dma_start(out_rows[:, :, c * CH : (c + 1) * CH], y[:])
+                planes(c, y[:], bank)
+
+        for step in SEQ:
+            if step[0] == "p":
+                weights(step[1], int(step[2]))
+            elif step[0] == "A":
+                scores(int(step[1]))
+            elif step[0] == "B":
+                values(int(step[1]))
+            elif step[0] == "O":
+                output(int(step[1]))
+            else:
+                quantise_z()
         for q in range(4):
             queue["QSQS"[q]].dma_start(out_2[0, 4 * q : 4 * q + 4, :].bitcast(I32), out_op[1][32 * q : 32 * q + 4, :].bitcast(I32))

from contextlib import ExitStack

import concourse.mybir as mybir
from concourse.masks import make_identity

K, T, S, H, N = 512, 2048, 512, 512, 512
FLOPS = 2 * K * S * H + 2 * K * S * N + 2 * S * H * N

F32 = mybir.dt.float32
BF16 = mybir.dt.bfloat16
I32 = mybir.dt.int32
U32 = mybir.dt.uint32
U16 = mybir.dt.uint16
U8 = mybir.dt.uint8
FP8X4 = mybir.dt.float8_e4m3fn_x4
ACT = mybir.ActivationFunctionType
ALU = mybir.AluOpType

P = 128
PACK = 4
CH = 128
HALF = 256
OUT_SCALE = 0.03125
CAST_A = "SSVV"
CAST_B = "VVSS"
Z2 = "VSSS"
YENG = "SSSS"
YBF = "VVVV"
LOADS = ["a01","a23","b01","b23"]
HOLD = 2
SEQ = ["pa0","pa1","pa2","pa3","pb0","pb1","pb2","pb3","A0","A1","A2","A3","Z","B0","B1","B2","B3","O0","O1","O2","O3"]
WIDE = ""
PAIRS = "y"
QZ = 2


def tile_picked_expool_exp_po_kernel(tc, x_words, x_scales, wa, wb, gt, gi, offs, out_0, out_1, out_2):
    nc = tc.nc
    with ExitStack() as ctx:
        keep = ctx.enter_context(tc.tile_pool(name="keep", bufs=1))
        psum = ctx.enter_context(tc.psum_pool(name="psum", bufs=8))
        queue = {"Q": nc.sync, "S": nc.scalar}

        def sb(name, shape, dtype):
            return keep.tile(shape, dtype, name=name, align_bytes=64)

        offsets = keep.tile([P, S // 16], U16, name="offsets")
        nc.sync.dma_start(offsets[:], offs)

        table_scales = sb("table_scales", [P, T], U8)
        nc.vector.memset(table_scales[:].bitcast(I32), 0)
        table_words = sb("table_words", [P, T], U32)
        words_in = x_words[0].rearrange("p n t -> p (n t)").bitcast(I32)
        nc.sync.dma_start(table_words[:, 0 : T // 4].bitcast(I32), words_in[:, 0 : T // 4])
        for e in range(2):
            nc.sync.dma_start(table_scales[e:P:16, :].bitcast(I32), x_scales[0, e:16:2, :].bitcast(I32))

        gates = sb("gates", [P, 2, 32], F32)
        for i, gate in enumerate((gt, gi)):
            nc.scalar.dma_start(gates[:, i, :], gate.rearrange("(b k) o -> b (k o)", k=32).unsqueeze(1).to_broadcast([16, 8, 32]))

        nc.sync.dma_start(table_words[:, T // 4 : T].bitcast(I32), words_in[:, T // 4 : T])

        raw = {}

        def load(group, dst):
            w = {"a": wa, "b": wb}[group[0]]
            first, count = int(group[1]), len(group) - 1
            nc.sync.dma_start(dst, w.rearrange("(p j) n -> p j n", j=PACK)[:, :, first * CH : (first + count) * CH])
            for i in range(count):
                raw[group[0], first + i] = dst[:, :, i * CH : (i + 1) * CH]

        for group in LOADS[:HOLD]:
            load(group, sb("raw_" + group, [P, PACK, (len(group) - 1) * CH], F32)[:])

        warm = sb("warm", [P, 1], F32)
        nc.scalar.activation(warm[:], gates[:, 0, 0:1], ACT.Exp, scale=0.0)

        identity = sb("identity", [P, P], F32)
        make_identity(nc, identity[:])
        own = sb("own", [P, 8], F32)
        nc.vector.tensor_reduce(own[:], identity[:].rearrange("p (b r) -> p r b", r=8), mybir.AxisListType.X, ALU.add)
        masked = sb("masked", [P, 2 * PACK, 8], F32)
        nc.vector.tensor_tensor(
            masked[:], gates[:].rearrange("p s (t r) -> p (s t) r", r=8), own[:].unsqueeze(1).to_broadcast([P, 2 * PACK, 8]), ALU.mult
        )
        dealt = sb("dealt", [P, 2 * PACK], F32)
        nc.vector.tensor_reduce(dealt[:], masked[:], mybir.AxisListType.X, ALU.add)
        gt_sb = dealt[:, 0:PACK]
        gi_sb = dealt[:, PACK : 2 * PACK]

        picked_scales = keep.tile([P, S], U8, name="picked_scales", tag="late", align_bytes=64)
        nc.vector.tensor_copy(picked_scales[:], table_scales[:].indirect(offsets[:]))
        x_sc = sb("x_sc", [P, S], U8)
        nc.vector.tensor_copy(
            x_sc[:].bitcast(I32).rearrange("p (t b w) -> p t b w", t=PACK, w=2),
            picked_scales[:].bitcast(I32).rearrange("p (b t w) -> p t b w", t=PACK, w=2),
        )
        for e in range(2):
            queue["Q"].dma_start(x_sc[2 + e : P : 32, :].bitcast(I32), x_sc[16 + e : P : 32, :].bitcast(I32))

        late_chunks = sum(len(group) - 1 for group in LOADS[HOLD:])
        late = keep.tile([P, late_chunks * PACK * CH], F32, name="late", tag="late", align_bytes=64)
        at = 0
        for group in LOADS[HOLD:]:
            size = (len(group) - 1) * PACK * CH
            load(group, late[:, at : at + size].rearrange("p (j n) -> p j n", j=PACK))
            at = at + size

        picked_words = sb("picked_words", [P, S], U32)
        nc.vector.tensor_copy(picked_words[:], table_words[:].indirect(offsets[:]))
        x_codes = sb("x_codes", [P, S], U32)
        nc.vector.tensor_copy(
            x_codes[:].rearrange("p (t b r) -> p t b r", t=PACK, r=8), picked_words[:].rearrange("p (b t r) -> p t b r", t=PACK, r=8)
        )

        def operand(name, width):
            return sb(name + "_codes", [P, width], U32), sb(name + "_scales", [P, width], U8)

        def quantise(op, cols, values):
            nc.vector.quantize_mx(out=op[0][:, cols].bitcast(FP8X4), scales=op[1][:, cols], in_=values)

        def interleave(engine, dst, src):
            dst_v = dst.rearrange("p (c i) j -> p c j i", i=4)
            src_v = src.rearrange("p j (c i) -> p c j i", i=4)
            if engine == "S":
                nc.scalar.copy(dst_v, src_v)
            else:
                nc.vector.tensor_copy(dst_v, src_v)

        def products(lhs, tiles, rhs, width):
            bank = psum.tile([P, len(tiles), width], F32, name="bank")
            for i, t in enumerate(tiles):
                nc.tensor.matmul_mx(
                    out=bank[:, i, :],
                    lhsT=lhs[0][:, t * P : (t + 1) * P].bitcast(FP8X4),
                    lhsT_scale=lhs[1][:, t * P : (t + 1) * P],
                    rhs=rhs[0].bitcast(FP8X4),
                    rhs_scale=rhs[1],
                    start=True,
                    stop=True,
                )
            return bank

        w_ops = {}
        w_bfs = {}

        def weights(name, c):
            engine = {"a": CAST_A, "b": CAST_B}[name][c]
            if name in PAIRS:
                if c % 2 == 0:
                    w_bfs[name, c // 2] = sb("w%s_bf%d" % (name, c), [P, HALF, PACK], BF16)
                w_bf = w_bfs[name, c // 2]
                interleave(engine, w_bf[:, (c % 2) * CH : (c % 2 + 1) * CH, :], raw[name, c])
                if c % 2 == 1:
                    op = operand("w%s%d" % (name, c), HALF)
                    quantise(op, slice(0, HALF), w_bf[:].rearrange("p n j -> p (n j)"))
                    w_ops[name, c - 1] = (op[0][:, 0:CH], op[1][:, 0:CH])
                    w_ops[name, c] = (op[0][:, CH:HALF], op[1][:, CH:HALF])
            else:
                w_bf = sb("w%s_bf%d" % (name, c), [P, CH, PACK], BF16)
                interleave(engine, w_bf[:], raw[name, c])
                op = operand("w%s%d" % (name, c), CH)
                quantise(op, slice(0, CH), w_bf[:].rearrange("p n j -> p (n j)"))
                w_ops[name, c] = (op[0][:], op[1][:])

        x_op = (x_codes, x_sc)
        z_bf = sb("z_bf", [P, PACK, P, PACK], BF16)
        z_op = operand("z", H)
        z2_ops = [operand("z2_%d" % h, HALF) for h in range(2)]
        out_op = operand("out", N)
        out_rows = out_0.rearrange("(p u) n -> p u n", u=PACK)
        words_out = out_1[0].rearrange("p n t -> p (n t)").bitcast(I32)
        y_bfs = {}

        def scores(c):
            bank = products(x_op, range(PACK), w_ops["a", c], CH)
            e_sb = sb("e%d" % c, [P, PACK, CH // PACK, PACK], F32)
            nc.scalar.activation(e_sb[:], bank[:].rearrange("p t (m u) -> p u m t", u=PACK), ACT.Exp, scale=0.5)
            m0 = c * (CH // PACK)
            nc.vector.tensor_tensor(
                z_bf[:, :, m0 : m0 + CH // PACK, :],
                e_sb[:],
                gt_sb.unsqueeze(1).unsqueeze(1).to_broadcast([P, PACK, CH // PACK, PACK]),
                ALU.mult,
            )

        def quantise_z():
            n = PACK // QZ
            for g in range(QZ):
                quantise(z_op, slice(g * n * P, (g + 1) * n * P), z_bf[:, n * g : n * g + n].rearrange("p u m t -> p (u m t)"))

        def values(c):
            bank = products(x_op, range(PACK), w_ops["b", c], CH)
            z2_bf = sb("z2_bf%d" % c, [P, CH, PACK], BF16)
            if Z2[c] == "V":
                nc.vector.tensor_tensor(
                    z2_bf[:],
                    bank[:].rearrange("p t n -> p n t"),
                    gi_sb.unsqueeze(1).to_broadcast([P, CH, PACK]),
                    ALU.mult,
                )
            else:
                rows = sb("z2_rows%d" % c, [P, PACK, CH], BF16)
                for t in range(PACK):
                    nc.scalar.activation(rows[:, t, :], bank[:, t, :], ACT.Copy, scale=gi_sb[:, t : t + 1])
                interleave("V", z2_bf[:], rows[:])
            quantise(z2_ops[c // 2], slice((c % 2) * CH, (c % 2 + 1) * CH), z2_bf[:].rearrange("p n t -> p (n t)"))

        def scaled(engine, dst, src):
            if engine == "S":
                nc.scalar.activation(dst, src, ACT.Copy, scale=OUT_SCALE)
            else:
                nc.vector.tensor_scalar(dst, src, OUT_SCALE, None, ALU.mult)

        def planes(c, y, bank):
            h = c // 2
            half = slice(h * HALF, (h + 1) * HALF)
            if "y" in PAIRS:
                if c % 2 == 0:
                    y_bfs[h] = sb("y_bf%d" % c, [P, HALF, PACK], BF16)
                dst = y_bfs[h][:, (c % 2) * CH : (c % 2 + 1) * CH, :]
            else:
                dst = sb("y_bf%d" % c, [P, CH, PACK], BF16)[:]
            if YBF[c] == "S" and bank is not None:
                scaled("S", dst, bank[:].rearrange("p u n -> p n u"))
            else:
                interleave(YBF[c], dst, y)
            if "y" not in PAIRS:
                quantise(out_op, slice(c * CH, (c + 1) * CH), dst.rearrange("p n u -> p (n u)"))
            elif c % 2 == 1:
                quantise(out_op, half, y_bfs[h][:].rearrange("p n u -> p (n u)"))
            if c % 2 == 1:
                queue["SS"[h]].dma_start(words_out[:, half], out_op[0][:, half].bitcast(I32))

        def output(c):
            h = c // 2
            if str(h) in WIDE:
                if c % 2 == 0:
                    return
                y = sb("y%d" % c, [P, PACK, HALF], F32)
                for g in range(2):
                    pair = slice(2 * g, 2 * g + 2)
                    bank = products(z_op, range(2 * g, 2 * g + 2), (z2_ops[h][0][:], z2_ops[h][1][:]), HALF)
                    scaled(YENG[2 * h + g], y[:, pair, :], bank[:])
                    queue["QQQQ"[2 * h + g]].dma_start(out_rows[:, pair, h * HALF : (h + 1) * HALF], y[:, pair, :])
                for k in range(2):
                    planes(2 * h + k, y[:, :, k * CH : (k + 1) * CH], None)
            else:
                cols = slice((c % 2) * CH, (c % 2 + 1) * CH)
                bank = products(z_op, range(PACK), (z2_ops[h][0][:, cols], z2_ops[h][1][:, cols]), CH)
                y = sb("y%d" % c, [P, PACK, CH], F32)
                scaled(YENG[c], y[:], bank[:])
                queue["QQQQ"[c]].dma_start(out_rows[:, :, c * CH : (c + 1) * CH], y[:])
                planes(c, y[:], bank)

        for step in SEQ:
            if step[0] == "p":
                weights(step[1], int(step[2]))
            elif step[0] == "A":
                scores(int(step[1]))
            elif step[0] == "B":
                values(int(step[1]))
            elif step[0] == "O":
                output(int(step[1]))
            else:
                quantise_z()
        for q in range(4):
            queue["QSQS"[q]].dma_start(out_2[0, 4 * q : 4 * q + 4, :].bitcast(I32), out_op[1][32 * q : 32 * q + 4, :].bitcast(I32))
